import numpy as np
import ml_dtypes


def mxq(x, axis, fmt="e4m3"):
    dtype, down = {"e4m3": (ml_dtypes.float8_e4m3fn, 7), "e5m2": (ml_dtypes.float8_e5m2, 14)}[fmt]
    v = np.moveaxis(np.asarray(x, np.float32).astype(ml_dtypes.bfloat16).astype(np.float64), axis, -1)
    blocks = v.reshape(v.shape[:-1] + (-1, 32))
    amax = np.abs(blocks).max(-1, keepdims=True)
    byte = np.maximum(np.where(amax > 0, np.frexp(amax)[1] - 1 + 127, 0) - down, 1)
    scale = np.exp2(byte - 127.0)
    codes = (blocks / scale).astype(np.float32).astype(dtype).astype(np.float64)
    return np.moveaxis((codes * scale).reshape(v.shape), -1, axis)


WIDE = False


def mx_kscale(k):
    if not WIDE:
        return np.ones(k)
    levels = np.array([10, -10, 5, -5, 0])
    if k % 512:
        return np.exp2(np.random.permutation(np.resize(levels, k // 32))).repeat(32)
    a = np.empty((k // 512, 16))
    for p in range(k // 512):
        a[p, :8] = np.random.permutation(np.resize(levels, 8))
        for g in range(8):
            far = levels[np.abs(levels - a[p, g]) >= 10]
            a[p, g + 8] = far[np.random.randint(len(far))]
    return np.exp2(a.ravel()).repeat(32)


def f64(x):
    return np.asarray(x).astype(np.float64)


def striped(idx):
    return np.tile(idx.reshape(-1, 16).T, (8, 1)).astype(np.uint16)


def unstriped(offs):
    return offs[:16].T.reshape(-1).astype(np.int64)


E2M1 = np.array([0.0, 0.5, 1.0, 1.5, 2.0, 3.0, 4.0, 6.0, -0.0, -0.5, -1.0, -1.5, -2.0, -3.0, -4.0, -6.0])


def pack_weight(w, fmt):
    k, n = w.shape
    w = f64(np.asarray(w, np.float32).astype(ml_dtypes.bfloat16)).reshape(k // 32, 32, n)
    amax = np.abs(w).max(1)
    if fmt == "e4m3":
        byte = np.frexp(amax)[1] - 1 + 127 - 7
    else:
        mant, ex = np.frexp(amax / 6.0)
        byte = np.where(mant > 0.5, ex, ex - 1) + 127
    byte = np.clip(np.where(amax > 0, byte, 1), 1, 254)
    scaled = (w * np.exp2(127.0 - byte)[:, None, :]).reshape(k, n).astype(np.float32)
    by_word = np.ascontiguousarray(scaled.reshape(k // 512, 128, 4, n).transpose(0, 1, 3, 2))
    if fmt == "e4m3":
        words = by_word.astype(ml_dtypes.float8_e4m3fn).view(np.uint8)
    else:
        c = by_word.astype(ml_dtypes.float4_e2m1fn).view(np.uint8) & 0xF
        words = (c[..., 0::2] | (c[..., 1::2] << 4)).reshape(k // 512, 128, 2 * n)
    return np.ascontiguousarray(words), np.ascontiguousarray(byte.astype(np.uint8).reshape(k // 512, 16, n))


def unpack_weight(words, scales, fmt):
    g, _, n = scales.shape
    words = np.ascontiguousarray(words).reshape(g, 128, n, -1)
    if fmt == "e4m3":
        vals = words.view(ml_dtypes.float8_e4m3fn).astype(np.float64)
    else:
        nib = np.empty((g, 128, n, 4), np.uint8)
        nib[..., 0::2] = words & 0xF
        nib[..., 1::2] = words >> 4
        vals = E2M1[nib]
    vals = vals * np.repeat(np.exp2(scales.astype(np.float64) - 127.0), 8, axis=1)[..., None]
    return vals.transpose(0, 1, 3, 2).reshape(g * 512, n)


def relu(v):
    return np.maximum(v, 0.0)


K, T, E, C, H, N = 512, 3072, 8, 256, 512, 256


def by_expert(wq, xq):
    return np.concatenate([wq[e].T @ xq[:, e * C:(e + 1) * C] for e in range(E)], axis=1)


def setup_inputs():
    n = np.random.standard_normal
    s = mx_kscale(K)[:, None]
    u = mx_kscale(H)
    x = pack_weight(n((K, T)) * s, "e4m3")
    return {
        "x_words": x[0],
        "x_scales": x[1],
        "xr": n((N, T)).astype(np.float32),
        "w1": (n((E, K, H)) / np.sqrt(K) / s[None]).astype(np.float32),
        "w3": (n((E, K, H)) / np.sqrt(K) / s[None] * u[None, None, :]).astype(np.float32),
        "w2": (n((E, H, N)) / np.sqrt(H) / u[None, :, None]).astype(np.float32),
        "gate": np.tile(np.random.uniform(0.2, 1.0, E * C), (N, 1)).astype(np.float32),
        "offs": striped(np.random.permutation(T)[:E * C]),
    }


def reference(x_words, x_scales, xr, w1, w3, w2, gate, offs):
    idx = unstriped(offs)
    xq = unpack_weight(x_words, x_scales, "e4m3")[:, idx]
    h = relu(by_expert(mxq(f64(w1), 1, "e4m3"), xq))
    h = h * by_expert(mxq(f64(w3), 1, "e4m3"), xq)
    y = by_expert(mxq(f64(w2), 1, "e4m3"), mxq(h, 0, "e4m3"))
    out = f64(xr).copy()
    out[:, idx] += f64(gate) * y
    return out

@@ -1,0 +1,212 @@
+from contextlib import ExitStack
+
+import concourse.mybir as mybir
+
+K, T, E, C, H, N = 512, 3072, 8, 256, 512, 256
+SLOTS = E * C
+FLOPS = 2 * SLOTS * (2 * K * H + H * N)
+
+F32 = mybir.dt.float32
+BF16 = mybir.dt.bfloat16
+I32 = mybir.dt.int32
+U32 = mybir.dt.uint32
+U16 = mybir.dt.uint16
+U8 = mybir.dt.uint8
+FP8X4 = mybir.dt.float8_e4m3fn_x4
+MULT = mybir.AluOpType.mult
+ADD = mybir.AluOpType.add
+RELU = mybir.ActivationFunctionType.Relu
+
+P = 128
+PACK = 4
+HALF = 128
+LIST_ROWS = 16
+GATHER = 1024
+SCATTER_ENDS = ((512, 1024, 1536, 2048), (768, 1280, 1664, 2048))
+W2_CASTS_ON_VECTOR = 4
+RAW_COLS = 2048
+ADD_COLS = 1024
+
+
+def tile_moe_res_glu_relu_kernel(
+    tc, x_words, x_scales, xr, w1, w3, w2, gate, offs, out
+):
+    nc = tc.nc
+    with ExitStack() as ctx:
+        held = ctx.enter_context(tc.tile_pool(name="held", bufs=1))
+        stream = ctx.enter_context(tc.tile_pool(name="stream", bufs=1))
+        psum = ctx.enter_context(tc.psum_pool(name="psum", bufs=1))
+
+        offsets = held.tile([P, SLOTS // LIST_ROWS], U16, name="offsets")
+        tok_words = held.tile([P, T], I32, name="tok_words")
+        tok_scales = held.tile([P, T], U8, name="tok_scales")
+        windows = [held.tile([P, T], F32, name=f"window{nb}") for nb in range(2)]
+        gates = held.tile([P, SLOTS], F32, name="gates")
+        y_slots = held.tile([P, 2, SLOTS], F32, name="y_slots")
+
+        nc.gpsimd.memset(tok_scales[:].bitcast(I32), 0)
+        for nb in range(2):
+            nc.gpsimd.memset(windows[nb][:], 0.0)
+
+        nc.sync.dma_start(offsets[:], offs)
+        nc.sync.dma_start(tok_words[:], x_words[0].rearrange("p t r -> p (t r)").bitcast(I32))
+        for r in range(4):
+            nc.sync.dma_start(tok_scales[r:P:32, :].bitcast(I32), x_scales[0, r:16:4, :].bitcast(I32))
+
+        def raw_tile(name):
+            return stream.tile([P, RAW_COLS], F32, name=name, tag="raw", bufs=11)
+
+        def list_cols(lo, hi):
+            return offsets[:, lo // LIST_ROWS : hi // LIST_ROWS]
+
+        raw = {}
+
+        def load(e):
+            for name, w in (("w1", w1), ("w3", w3)):
+                raw[name, e] = raw_tile(f"raw_{name}")
+                nc.sync.dma_start(raw[name, e][:], w[e].rearrange("(p j) h -> p (j h)", j=PACK))
+
+        def load_second(e):
+            raw["w2", e] = stream.tile([P, PACK, N], F32, name="raw_w2", bufs=4)
+            rows = w2[e].rearrange("(m t b) n -> b m t n", t=PACK, b=2)
+            for b in range(2):
+                nc.sync.dma_start(raw["w2", e][b:P:2, :, :], rows[b])
+            if e % 2 == 1:
+                cols = slice((e - 1) * C, (e + 1) * C)
+                nc.sync.dma_start(gates[:, cols], gate[0:P, cols])
+
+        gathered = {}
+
+        def gather(g):
+            words = held.tile([P, GATHER], I32, name=f"slot_words{g}", align_bytes=64)
+            scales = held.tile([P, GATHER], U8, name=f"slot_scales{g}", align_bytes=64)
+            cols = list_cols(g * GATHER, (g + 1) * GATHER)
+            nc.vector.tensor_copy(words[:].bitcast(U32), tok_words[:].bitcast(U32).indirect(cols))
+            nc.vector.tensor_copy(scales[:], tok_scales[:].indirect(cols))
+            gathered[g] = (words, scales)
+
+        def quantise(src, width, tag, bufs):
+            codes = stream.tile([P, width], U32, name=f"codes_{tag}", bufs=bufs, align_bytes=64)
+            scales = stream.tile([P, width], U8, name=f"scales_{tag}", bufs=bufs, align_bytes=64)
+            nc.vector.quantize_mx(out=codes[:].bitcast(FP8X4), scales=scales[:], in_=src)
+            return codes, scales
+
+        quant = {}
+
+        def prepare(e):
+            for name in ("w1", "w3"):
+                rounded = stream.tile([P, PACK * H], BF16, name=f"rounded_{name}", bufs=2, align_bytes=64)
+                nc.scalar.copy(
+                    rounded[:].rearrange("p (t m b j) -> p m t j b", t=PACK, b=2, j=PACK),
+                    raw[name, e][:].rearrange("p (j m t b) -> p m t j b", j=PACK, t=PACK, b=2),
+                )
+                quant[name, e] = quantise(rounded[:], H, "w13", 4)
+            rounded = stream.tile([P, PACK * N], BF16, name="rounded_w2", bufs=2, align_bytes=64)
+            dst = rounded[:].rearrange("p (c b t) -> p c t b", b=2, t=PACK)
+            src = raw["w2", e][:].rearrange("p t (c b) -> p c t b", b=2)
+            if e < W2_CASTS_ON_VECTOR:
+                nc.vector.tensor_copy(dst, src)
+            else:
+                nc.scalar.copy(dst, src)
+            quant["w2", e] = quantise(rounded[:], N, "w2", 3)
+
+        def matmul(acc, lhs, lhs_cols, rhs, rhs_cols):
+            nc.tensor.matmul_mx(
+                out=acc,
+                lhsT=lhs[0][:, lhs_cols].bitcast(FP8X4),
+                lhsT_scale=lhs[1][:, lhs_cols],
+                rhs=rhs[0][:, rhs_cols].bitcast(FP8X4),
+                rhs_scale=rhs[1][:, rhs_cols],
+                start=True,
+                stop=True,
+            )
+
+        def first_layer(e):
+            tokens = gathered[e * C // GATHER]
+            banks = {}
+            for name, bufs in (("w1", 2), ("w3", 4)):
+                for u in range(C // HALF):
+                    first = e * C % GATHER + u * HALF
+                    banks[name, u] = psum.tile([P, PACK, HALF], F32, name=f"acc_{name}", bufs=bufs)
+                    for t in range(PACK):
+                        matmul(banks[name, u][:, t, :], quant[name, e], slice(t * P, (t + 1) * P),
+                               tokens, slice(first, first + HALF))
+            return banks
+
+        def activate(e, banks):
+            room = raw["w3", e + 1] if e + 1 < E else raw["w1", e]
+            pairs = []
+            for u in range(C // HALF):
+                active = room[:, u * HALF * PACK : (u + 1) * HALF * PACK].rearrange("p (c t) -> p c t", t=PACK)
+                nc.scalar.activation(active, banks["w1", u][:].rearrange("p t c -> p c t"), RELU)
+                pairs.append((active, banks["w3", u]))
+            return pairs
+
+        def second_layer(e, pairs):
+            hidden = stream.tile([P, C * PACK], BF16, name="hidden", bufs=2, align_bytes=64)
+            for u, (active, bank) in enumerate(pairs):
+                nc.vector.tensor_tensor(
+                    hidden[:, u * HALF * PACK : (u + 1) * HALF * PACK].rearrange("p (c t) -> p c t", t=PACK),
+                    bank[:].rearrange("p t c -> p c t"),
+                    active,
+                    MULT,
+                )
+            hq = quantise(hidden[:], C, "h", 2)
+            acc = psum.tile([P, 2, C], F32, name="acc_y", bufs=2)
+            for nb in range(2):
+                matmul(acc[:, nb, :], quant["w2", e], slice(nb * P, (nb + 1) * P), hq, slice(0, C))
+            return acc
+
+        def scatter(nb, lo, hi):
+            nc.vector.tensor_tensor(
+                windows[nb][:].indirect(list_cols(lo, hi)), y_slots[:, nb, lo:hi], gates[:, lo:hi], MULT
+            )
+
+        load(0)
+        load(1)
+        load_second(0)
+        load_second(1)
+        for e in range(2, E):
+            load(e)
+            load_second(e)
+        residual = []
+        for q in range(3):
+            tile_q = raw_tile("raw_xr")
+            residual.append(tile_q)
+            for s in range(2):
+                nb, c = divmod(2 * q + s, 3)
+                nc.sync.dma_start(
+                    tile_q[:, s * ADD_COLS : (s + 1) * ADD_COLS],
+                    xr[nb * P : (nb + 1) * P, c * ADD_COLS : (c + 1) * ADD_COLS],
+                )
+
+        for g in range(SLOTS // GATHER):
+            gather(g)
+        prepare(0)
+        done = [0, 0]
+        sums = {}
+
+        def bring_back(e):
+            nc.scalar.copy(y_slots[:, :, e * C : (e + 1) * C], sums[e][:])
+            for nb in range(2):
+                for hi in SCATTER_ENDS[nb][:-1]:
+                    if done[nb] < hi <= (e + 1) * C:
+                        scatter(nb, done[nb], hi)
+                        done[nb] = hi
+
+        for e in range(E):
+            banks = first_layer(e)
+            if e + 1 < E:
+                prepare(e + 1)
+            sums[e] = second_layer(e, activate(e, banks))
+            if e > 0:
+                bring_back(e - 1)
+        bring_back(E - 1)
+        for nb in (1, 0):
+            scatter(nb, done[nb], SLOTS)
+            for c in range(3):
+                q, s = divmod(3 * nb + c, 2)
+                res = residual[q][:, s * ADD_COLS : (s + 1) * ADD_COLS]
+                cols = slice(c * ADD_COLS, (c + 1) * ADD_COLS)
+                nc.vector.tensor_tensor(res, res, windows[nb][:, cols], ADD)
+                nc.sync.dma_start(out[nb * P : (nb + 1) * P, cols], res)

@@ -23,7 +23,8 @@ HALF = 128
 LIST_ROWS = 16
 GATHER = 1024
 SCATTER_ENDS = ((512, 1024, 1536, 2048), (768, 1280, 1664, 2048))
-W2_CASTS_ON_VECTOR = 4
+W2_CASTS_ON_VECTOR = 6
+ADD_CUTS = (0, 1024, 2048, 3072)
 RAW_COLS = 2048
 ADD_COLS = 1024
 
@@ -45,13 +46,20 @@ def tile_moe_res_glu_relu_kernel(
         y_slots = held.tile([P, 2, SLOTS], F32, name="y_slots")
 
         nc.gpsimd.memset(tok_scales[:].bitcast(I32), 0)
+        zero = held.tile([P, 1], F32, name="zero")
+        nc.gpsimd.memset(zero[:], 0.0)
         for nb in range(2):
-            nc.gpsimd.memset(windows[nb][:], 0.0)
+            nc.scalar.copy(windows[nb][:], zero[:].to_broadcast([P, T]))
+
+        def load_gates(pair):
+            cols = slice(2 * pair * C, 2 * (pair + 1) * C)
+            nc.sync.dma_start(gates[:, cols], gate[0:P, cols])
 
         nc.sync.dma_start(offsets[:], offs)
-        nc.sync.dma_start(tok_words[:], x_words[0].rearrange("p t r -> p (t r)").bitcast(I32))
+        load_gates(0)
         for r in range(4):
             nc.sync.dma_start(tok_scales[r:P:32, :].bitcast(I32), x_scales[0, r:16:4, :].bitcast(I32))
+        nc.sync.dma_start(tok_words[:], x_words[0].rearrange("p t r -> p (t r)").bitcast(I32))
 
         def raw_tile(name):
             return stream.tile([P, RAW_COLS], F32, name=name, tag="raw", bufs=11)
@@ -71,19 +79,21 @@ def tile_moe_res_glu_relu_kernel(
             rows = w2[e].rearrange("(m t b) n -> b m t n", t=PACK, b=2)
             for b in range(2):
                 nc.sync.dma_start(raw["w2", e][b:P:2, :, :], rows[b])
-            if e % 2 == 1:
-                cols = slice((e - 1) * C, (e + 1) * C)
-                nc.sync.dma_start(gates[:, cols], gate[0:P, cols])
+            if e % 2 == 1 and e > 1:
+                load_gates(e // 2)
 
         gathered = {}
 
-        def gather(g):
-            words = held.tile([P, GATHER], I32, name=f"slot_words{g}", align_bytes=64)
-            scales = held.tile([P, GATHER], U8, name=f"slot_scales{g}", align_bytes=64)
-            cols = list_cols(g * GATHER, (g + 1) * GATHER)
-            nc.vector.tensor_copy(words[:].bitcast(U32), tok_words[:].bitcast(U32).indirect(cols))
-            nc.vector.tensor_copy(scales[:], tok_scales[:].indirect(cols))
-            gathered[g] = (words, scales)
+        def gather_all():
+            parts = range(SLOTS // GATHER)
+            lists = [list_cols(g * GATHER, (g + 1) * GATHER) for g in parts]
+            words = [held.tile([P, GATHER], I32, name=f"slot_words{g}", align_bytes=64) for g in parts]
+            scales = [held.tile([P, GATHER], U8, name=f"slot_scales{g}", align_bytes=64) for g in parts]
+            for g in parts:
+                nc.vector.tensor_copy(scales[g][:], tok_scales[:].indirect(lists[g]))
+            for g in parts:
+                nc.vector.tensor_copy(words[g][:].bitcast(U32), tok_words[:].bitcast(U32).indirect(lists[g]))
+                gathered[g] = (words[g], scales[g])
 
         def quantise(src, width, tag, bufs):
             codes = stream.tile([P, width], U32, name=f"codes_{tag}", bufs=bufs, align_bytes=64)
@@ -93,14 +103,15 @@ def tile_moe_res_glu_relu_kernel(
 
         quant = {}
 
-        def prepare(e):
-            for name in ("w1", "w3"):
-                rounded = stream.tile([P, PACK * H], BF16, name=f"rounded_{name}", bufs=2, align_bytes=64)
-                nc.scalar.copy(
-                    rounded[:].rearrange("p (t m b j) -> p m t j b", t=PACK, b=2, j=PACK),
-                    raw[name, e][:].rearrange("p (j m t b) -> p m t j b", j=PACK, t=PACK, b=2),
-                )
-                quant[name, e] = quantise(rounded[:], H, "w13", 4)
+        def prepare(name, e):
+            rounded = stream.tile([P, PACK * H], BF16, name=f"rounded_{name}", bufs=2, align_bytes=64)
+            nc.scalar.copy(
+                rounded[:].rearrange("p (t m b j) -> p m t j b", t=PACK, b=2, j=PACK),
+                raw[name, e][:].rearrange("p (j m t b) -> p m t j b", j=PACK, t=PACK, b=2),
+            )
+            quant[name, e] = quantise(rounded[:], H, "w13", 4)
+
+        def prepare_second(e):
             rounded = stream.tile([P, PACK * N], BF16, name="rounded_w2", bufs=2, align_bytes=64)
             dst = rounded[:].rearrange("p (c b t) -> p c t b", b=2, t=PACK)
             src = raw["w2", e][:].rearrange("p t (c b) -> p c t b", b=2)
@@ -124,17 +135,17 @@ def tile_moe_res_glu_relu_kernel(
         def first_layer(e):
             tokens = gathered[e * C // GATHER]
             banks = {}
-            for name, bufs in (("w1", 2), ("w3", 4)):
+            for name in ("w1", "w3"):
                 for u in range(C // HALF):
                     first = e * C % GATHER + u * HALF
-                    banks[name, u] = psum.tile([P, PACK, HALF], F32, name=f"acc_{name}", bufs=bufs)
+                    banks[name, u] = psum.tile([P, PACK, HALF], F32, name=f"acc_{name}", bufs=4)
                     for t in range(PACK):
                         matmul(banks[name, u][:, t, :], quant[name, e], slice(t * P, (t + 1) * P),
                                tokens, slice(first, first + HALF))
             return banks
 
         def activate(e, banks):
-            room = raw["w3", e + 1] if e + 1 < E else raw["w1", e]
+            room = raw["w1", e + 1][:, 0 : C * PACK] if e + 1 < E else raw["w1", e][:, C * PACK : 2 * C * PACK]
             pairs = []
             for u in range(C // HALF):
                 active = room[:, u * HALF * PACK : (u + 1) * HALF * PACK].rearrange("p (c t) -> p c t", t=PACK)
@@ -142,7 +153,7 @@ def tile_moe_res_glu_relu_kernel(
                 pairs.append((active, banks["w3", u]))
             return pairs
 
-        def second_layer(e, pairs):
+        def hidden_codes(pairs):
             hidden = stream.tile([P, C * PACK], BF16, name="hidden", bufs=2, align_bytes=64)
             for u, (active, bank) in enumerate(pairs):
                 nc.vector.tensor_tensor(
@@ -151,24 +162,24 @@ def tile_moe_res_glu_relu_kernel(
                     active,
                     MULT,
                 )
-            hq = quantise(hidden[:], C, "h", 2)
-            acc = psum.tile([P, 2, C], F32, name="acc_y", bufs=2)
+            return quantise(hidden[:], C, "h", 3)
+
+        def second_layer(e, bank):
+            acc = bank[:].rearrange("p (nb a) c -> p nb (a c)", nb=2)
             for nb in range(2):
-                matmul(acc[:, nb, :], quant["w2", e], slice(nb * P, (nb + 1) * P), hq, slice(0, C))
-            return acc
+                matmul(acc[:, nb, :], quant["w2", e], slice(nb * P, (nb + 1) * P), quant["h", e], slice(0, C))
+            nc.scalar.copy(y_slots[:, :, e * C : (e + 1) * C], acc)
 
         def scatter(nb, lo, hi):
             nc.vector.tensor_tensor(
                 windows[nb][:].indirect(list_cols(lo, hi)), y_slots[:, nb, lo:hi], gates[:, lo:hi], MULT
             )
 
-        load(0)
-        load(1)
-        load_second(0)
-        load_second(1)
-        for e in range(2, E):
+        for e in range(E):
             load(e)
-            load_second(e)
+            if e > 0:
+                load_second(e - 1)
+        load_second(E - 1)
         residual = []
         for q in range(3):
             tile_q = raw_tile("raw_xr")
@@ -180,14 +191,12 @@ def tile_moe_res_glu_relu_kernel(
                     xr[nb * P : (nb + 1) * P, c * ADD_COLS : (c + 1) * ADD_COLS],
                 )
 
-        for g in range(SLOTS // GATHER):
-            gather(g)
-        prepare(0)
+        gather_all()
+        prepare("w1", 0)
+        prepare("w3", 0)
         done = [0, 0]
-        sums = {}
 
-        def bring_back(e):
-            nc.scalar.copy(y_slots[:, :, e * C : (e + 1) * C], sums[e][:])
+        def scatter_ready(e):
             for nb in range(2):
                 for hi in SCATTER_ENDS[nb][:-1]:
                     if done[nb] < hi <= (e + 1) * C:
@@ -197,16 +206,21 @@ def tile_moe_res_glu_relu_kernel(
         for e in range(E):
             banks = first_layer(e)
             if e + 1 < E:
-                prepare(e + 1)
-            sums[e] = second_layer(e, activate(e, banks))
+                prepare("w1", e + 1)
+            pairs = activate(e, banks)
+            if e + 1 < E:
+                prepare("w3", e + 1)
+            prepare_second(e)
             if e > 0:
-                bring_back(e - 1)
-        bring_back(E - 1)
+                second_layer(e - 1, banks["w1", 1])
+            quant["h", e] = hidden_codes(pairs)
+            if e > 0:
+                scatter_ready(e - 1)
+        second_layer(E - 1, psum.tile([P, PACK, HALF], F32, name="acc_w1", bufs=4))
         for nb in (1, 0):
             scatter(nb, done[nb], SLOTS)
-            for c in range(3):
-                q, s = divmod(3 * nb + c, 2)
-                res = residual[q][:, s * ADD_COLS : (s + 1) * ADD_COLS]
-                cols = slice(c * ADD_COLS, (c + 1) * ADD_COLS)
-                nc.vector.tensor_tensor(res, res, windows[nb][:, cols], ADD)
-                nc.sync.dma_start(out[nb * P : (nb + 1) * P, cols], res)
+            for lo, hi in zip(ADD_CUTS, ADD_CUTS[1:]):
+                q, at = divmod(nb * T + lo, RAW_COLS)
+                res = residual[q][:, at : at + hi - lo]
+                nc.vector.tensor_tensor(res, res, windows[nb][:, lo:hi], ADD)
+                nc.sync.dma_start(out[nb * P : (nb + 1) * P, lo:hi], res)

@@ -23,7 +23,9 @@ HALF = 128
 LIST_ROWS = 16
 GATHER = 1024
 SCATTER_ENDS = ((512, 1024, 1536, 2048), (768, 1280, 1664, 2048))
-W2_CASTS_ON_VECTOR = 6
+W2_CASTS_ON_VECTOR = 5
+W3_CASTS_ON_VECTOR = (1, 2)
+BANKS = {"w1": 2, "w3": 6}
 ADD_CUTS = (0, 1024, 2048, 3072)
 RAW_COLS = 2048
 ADD_COLS = 1024
@@ -105,10 +107,12 @@ def tile_moe_res_glu_relu_kernel(
 
         def prepare(name, e):
             rounded = stream.tile([P, PACK * H], BF16, name=f"rounded_{name}", bufs=2, align_bytes=64)
-            nc.scalar.copy(
-                rounded[:].rearrange("p (t m b j) -> p m t j b", t=PACK, b=2, j=PACK),
-                raw[name, e][:].rearrange("p (j m t b) -> p m t j b", j=PACK, t=PACK, b=2),
-            )
+            dst = rounded[:].rearrange("p (t m b j) -> p m t j b", t=PACK, b=2, j=PACK)
+            src = raw[name, e][:].rearrange("p (j m t b) -> p m t j b", j=PACK, t=PACK, b=2)
+            if name == "w3" and e in W3_CASTS_ON_VECTOR:
+                nc.vector.tensor_copy(dst, src)
+            else:
+                nc.scalar.copy(dst, src)
             quant[name, e] = quantise(rounded[:], H, "w13", 4)
 
         def prepare_second(e):
@@ -138,7 +142,7 @@ def tile_moe_res_glu_relu_kernel(
             for name in ("w1", "w3"):
                 for u in range(C // HALF):
                     first = e * C % GATHER + u * HALF
-                    banks[name, u] = psum.tile([P, PACK, HALF], F32, name=f"acc_{name}", bufs=4)
+                    banks[name, u] = psum.tile([P, PACK, HALF], F32, name=f"acc_{name}", bufs=BANKS[name])
                     for t in range(PACK):
                         matmul(banks[name, u][:, t, :], quant[name, e], slice(t * P, (t + 1) * P),
                                tokens, slice(first, first + HALF))
@@ -210,13 +214,13 @@ def tile_moe_res_glu_relu_kernel(
             pairs = activate(e, banks)
             if e + 1 < E:
                 prepare("w3", e + 1)
-            prepare_second(e)
             if e > 0:
-                second_layer(e - 1, banks["w1", 1])
+                second_layer(e - 1, banks["w1", 0])
+            prepare_second(e)
             quant["h", e] = hidden_codes(pairs)
             if e > 0:
                 scatter_ready(e - 1)
-        second_layer(E - 1, psum.tile([P, PACK, HALF], F32, name="acc_w1", bufs=4))
+        second_layer(E - 1, psum.tile([P, PACK, HALF], F32, name="acc_w1", bufs=BANKS["w1"]))
         for nb in (1, 0):
             scatter(nb, done[nb], SLOTS)
             for lo, hi in zip(ADD_CUTS, ADD_CUTS[1:]):

@@ -23,12 +23,10 @@ HALF = 128
 LIST_ROWS = 16
 GATHER = 1024
 SCATTER_ENDS = ((512, 1024, 1536, 2048), (768, 1280, 1664, 2048))
-W2_CASTS_ON_VECTOR = 5
-W3_CASTS_ON_VECTOR = (1, 2)
+W3_CASTS_ON_VECTOR = (1, 2, 3)
 BANKS = {"w1": 2, "w3": 6}
-ADD_CUTS = (0, 1024, 2048, 3072)
 RAW_COLS = 2048
-ADD_COLS = 1024
+ADD_COLS = 768
 
 
 def tile_moe_res_glu_relu_kernel(
@@ -57,12 +55,6 @@ def tile_moe_res_glu_relu_kernel(
             cols = slice(2 * pair * C, 2 * (pair + 1) * C)
             nc.sync.dma_start(gates[:, cols], gate[0:P, cols])
 
-        nc.sync.dma_start(offsets[:], offs)
-        load_gates(0)
-        for r in range(4):
-            nc.sync.dma_start(tok_scales[r:P:32, :].bitcast(I32), x_scales[0, r:16:4, :].bitcast(I32))
-        nc.sync.dma_start(tok_words[:], x_words[0].rearrange("p t r -> p (t r)").bitcast(I32))
-
         def raw_tile(name):
             return stream.tile([P, RAW_COLS], F32, name=name, tag="raw", bufs=11)
 
@@ -71,17 +63,17 @@ def tile_moe_res_glu_relu_kernel(
 
         raw = {}
 
-        def load(e):
-            for name, w in (("w1", w1), ("w3", w3)):
-                raw[name, e] = raw_tile(f"raw_{name}")
-                nc.sync.dma_start(raw[name, e][:], w[e].rearrange("(p j) h -> p (j h)", j=PACK))
+        def load(name, e):
+            raw[name, e] = raw_tile(f"raw_{name}")
+            w = w1 if name == "w1" else w3
+            nc.sync.dma_start(raw[name, e][:], w[e].rearrange("(p j) h -> p (j h)", j=PACK))
 
         def load_second(e):
             raw["w2", e] = stream.tile([P, PACK, N], F32, name="raw_w2", bufs=4)
             rows = w2[e].rearrange("(m t b) n -> b m t n", t=PACK, b=2)
             for b in range(2):
                 nc.sync.dma_start(raw["w2", e][b:P:2, :, :], rows[b])
-            if e % 2 == 1 and e > 1:
+            if e % 2 == 1:
                 load_gates(e // 2)
 
         gathered = {}
@@ -119,10 +111,7 @@ def tile_moe_res_glu_relu_kernel(
             rounded = stream.tile([P, PACK * N], BF16, name="rounded_w2", bufs=2, align_bytes=64)
             dst = rounded[:].rearrange("p (c b t) -> p c t b", b=2, t=PACK)
             src = raw["w2", e][:].rearrange("p t (c b) -> p c t b", b=2)
-            if e < W2_CASTS_ON_VECTOR:
-                nc.vector.tensor_copy(dst, src)
-            else:
-                nc.scalar.copy(dst, src)
+            nc.scalar.copy(dst, src)
             quant["w2", e] = quantise(rounded[:], N, "w2", 3)
 
         def matmul(acc, lhs, lhs_cols, rhs, rhs_cols):
@@ -179,21 +168,23 @@ def tile_moe_res_glu_relu_kernel(
                 windows[nb][:].indirect(list_cols(lo, hi)), y_slots[:, nb, lo:hi], gates[:, lo:hi], MULT
             )
 
-        for e in range(E):
-            load(e)
-            if e > 0:
-                load_second(e - 1)
+        nc.sync.dma_start(offsets[:], offs)
+        load("w1", 0)
+        for r in range(4):
+            nc.sync.dma_start(tok_scales[r:P:32, :].bitcast(I32), x_scales[0, r:16:4, :].bitcast(I32))
+        nc.sync.dma_start(tok_words[:], x_words[0].rearrange("p t r -> p (t r)").bitcast(I32))
+        load("w3", 0)
+        for e in range(1, E):
+            load("w1", e)
+            load("w3", e)
+            load_second(e - 1)
         load_second(E - 1)
-        residual = []
-        for q in range(3):
-            tile_q = raw_tile("raw_xr")
-            residual.append(tile_q)
-            for s in range(2):
-                nb, c = divmod(2 * q + s, 3)
-                nc.sync.dma_start(
-                    tile_q[:, s * ADD_COLS : (s + 1) * ADD_COLS],
-                    xr[nb * P : (nb + 1) * P, c * ADD_COLS : (c + 1) * ADD_COLS],
-                )
+        residual = {}
+        for nb in (1, 0):
+            for half in range(2):
+                residual[nb, half] = raw_tile("raw_xr")
+                cols = slice(half * T // 2, (half + 1) * T // 2)
+                nc.sync.dma_start(residual[nb, half][:, 0 : T // 2], xr[nb * P : (nb + 1) * P, cols])
 
         gather_all()
         prepare("w1", 0)
@@ -223,8 +214,8 @@ def tile_moe_res_glu_relu_kernel(
         second_layer(E - 1, psum.tile([P, PACK, HALF], F32, name="acc_w1", bufs=BANKS["w1"]))
         for nb in (1, 0):
             scatter(nb, done[nb], SLOTS)
-            for lo, hi in zip(ADD_CUTS, ADD_CUTS[1:]):
-                q, at = divmod(nb * T + lo, RAW_COLS)
-                res = residual[q][:, at : at + hi - lo]
-                nc.vector.tensor_tensor(res, res, windows[nb][:, lo:hi], ADD)
-                nc.sync.dma_start(out[nb * P : (nb + 1) * P, lo:hi], res)
+            for lo in range(0, T, ADD_COLS):
+                half, at = divmod(lo, T // 2)
+                res = residual[nb, half][:, at : at + ADD_COLS]
+                nc.vector.tensor_tensor(res, res, windows[nb][:, lo : lo + ADD_COLS], ADD)
+                nc.sync.dma_start(out[nb * P : (nb + 1) * P, lo : lo + ADD_COLS], res)

from contextlib import ExitStack

import concourse.mybir as mybir

K, T, E, C, H, N = 512, 3072, 8, 256, 512, 256
SLOTS = E * C
FLOPS = 2 * SLOTS * (2 * K * H + H * N)

F32 = mybir.dt.float32
BF16 = mybir.dt.bfloat16
I32 = mybir.dt.int32
U32 = mybir.dt.uint32
U16 = mybir.dt.uint16
U8 = mybir.dt.uint8
FP8X4 = mybir.dt.float8_e4m3fn_x4
MULT = mybir.AluOpType.mult
ADD = mybir.AluOpType.add
RELU = mybir.ActivationFunctionType.Relu

P = 128
PACK = 4
HALF = 128
LIST_ROWS = 16
GATHER = 1024
SCATTER_ENDS = ((512, 1024, 1536, 2048), (768, 1280, 1664, 2048))
W3_CASTS_ON_VECTOR = (1, 2, 3)
BANKS = {"w1": 2, "w3": 6}
RAW_COLS = 2048
ADD_COLS = 768


def tile_moe_res_glu_relu_kernel(
    tc, x_words, x_scales, xr, w1, w3, w2, gate, offs, out
):
    nc = tc.nc
    with ExitStack() as ctx:
        held = ctx.enter_context(tc.tile_pool(name="held", bufs=1))
        stream = ctx.enter_context(tc.tile_pool(name="stream", bufs=1))
        psum = ctx.enter_context(tc.psum_pool(name="psum", bufs=1))

        offsets = held.tile([P, SLOTS // LIST_ROWS], U16, name="offsets")
        tok_words = held.tile([P, T], I32, name="tok_words")
        tok_scales = held.tile([P, T], U8, name="tok_scales")
        windows = [held.tile([P, T], F32, name=f"window{nb}") for nb in range(2)]
        gates = held.tile([P, SLOTS], F32, name="gates")
        y_slots = held.tile([P, 2, SLOTS], F32, name="y_slots")

        nc.gpsimd.memset(tok_scales[:].bitcast(I32), 0)
        zero = held.tile([P, 1], F32, name="zero")
        nc.gpsimd.memset(zero[:], 0.0)
        for nb in range(2):
            nc.scalar.copy(windows[nb][:], zero[:].to_broadcast([P, T]))

        def load_gates(pair):
            cols = slice(2 * pair * C, 2 * (pair + 1) * C)
            nc.sync.dma_start(gates[:, cols], gate[0:P, cols])

        def raw_tile(name):
            return stream.tile([P, RAW_COLS], F32, name=name, tag="raw", bufs=11)

        def list_cols(lo, hi):
            return offsets[:, lo // LIST_ROWS : hi // LIST_ROWS]

        raw = {}

        def load(name, e):
            raw[name, e] = raw_tile(f"raw_{name}")
            w = w1 if name == "w1" else w3
            nc.sync.dma_start(raw[name, e][:], w[e].rearrange("(p j) h -> p (j h)", j=PACK))

        def load_second(e):
            raw["w2", e] = stream.tile([P, PACK, N], F32, name="raw_w2", bufs=4)
            rows = w2[e].rearrange("(m t b) n -> b m t n", t=PACK, b=2)
            for b in range(2):
                nc.sync.dma_start(raw["w2", e][b:P:2, :, :], rows[b])
            if e % 2 == 1:
                load_gates(e // 2)

        gathered = {}

        def gather_all():
            parts = range(SLOTS // GATHER)
            lists = [list_cols(g * GATHER, (g + 1) * GATHER) for g in parts]
            words = [held.tile([P, GATHER], I32, name=f"slot_words{g}", align_bytes=64) for g in parts]
            scales = [held.tile([P, GATHER], U8, name=f"slot_scales{g}", align_bytes=64) for g in parts]
            for g in parts:
                nc.vector.tensor_copy(scales[g][:], tok_scales[:].indirect(lists[g]))
            for g in parts:
                nc.vector.tensor_copy(words[g][:].bitcast(U32), tok_words[:].bitcast(U32).indirect(lists[g]))
                gathered[g] = (words[g], scales[g])

        def quantise(src, width, tag, bufs):
            codes = stream.tile([P, width], U32, name=f"codes_{tag}", bufs=bufs, align_bytes=64)
            scales = stream.tile([P, width], U8, name=f"scales_{tag}", bufs=bufs, align_bytes=64)
            nc.vector.quantize_mx(out=codes[:].bitcast(FP8X4), scales=scales[:], in_=src)
            return codes, scales

        quant = {}

        def prepare(name, e):
            rounded = stream.tile([P, PACK * H], BF16, name=f"rounded_{name}", bufs=2, align_bytes=64)
            dst = rounded[:].rearrange("p (t m b j) -> p m t j b", t=PACK, b=2, j=PACK)
            src = raw[name, e][:].rearrange("p (j m t b) -> p m t j b", j=PACK, t=PACK, b=2)
            if name == "w3" and e in W3_CASTS_ON_VECTOR:
                nc.vector.tensor_copy(dst, src)
            else:
                nc.scalar.copy(dst, src)
            quant[name, e] = quantise(rounded[:], H, "w13", 4)

        def prepare_second(e):
            rounded = stream.tile([P, PACK * N], BF16, name="rounded_w2", bufs=2, align_bytes=64)
            dst = rounded[:].rearrange("p (c b t) -> p c t b", b=2, t=PACK)
            src = raw["w2", e][:].rearrange("p t (c b) -> p c t b", b=2)
            nc.scalar.copy(dst, src)
            quant["w2", e] = quantise(rounded[:], N, "w2", 3)

        def matmul(acc, lhs, lhs_cols, rhs, rhs_cols):
            nc.tensor.matmul_mx(
                out=acc,
                lhsT=lhs[0][:, lhs_cols].bitcast(FP8X4),
                lhsT_scale=lhs[1][:, lhs_cols],
                rhs=rhs[0][:, rhs_cols].bitcast(FP8X4),
                rhs_scale=rhs[1][:, rhs_cols],
                start=True,
                stop=True,
            )

        def first_layer(e):
            tokens = gathered[e * C // GATHER]
            banks = {}
            for name in ("w1", "w3"):
                for u in range(C // HALF):
                    first = e * C % GATHER + u * HALF
                    banks[name, u] = psum.tile([P, PACK, HALF], F32, name=f"acc_{name}", bufs=BANKS[name])
                    for t in range(PACK):
                        matmul(banks[name, u][:, t, :], quant[name, e], slice(t * P, (t + 1) * P),
                               tokens, slice(first, first + HALF))
            return banks

        def activate(e, banks):
            room = raw["w1", e + 1][:, 0 : C * PACK] if e + 1 < E else raw["w1", e][:, C * PACK : 2 * C * PACK]
            pairs = []
            for u in range(C // HALF):
                active = room[:, u * HALF * PACK : (u + 1) * HALF * PACK].rearrange("p (c t) -> p c t", t=PACK)
                nc.scalar.activation(active, banks["w1", u][:].rearrange("p t c -> p c t"), RELU)
                pairs.append((active, banks["w3", u]))
            return pairs

        def hidden_codes(pairs):
            hidden = stream.tile([P, C * PACK], BF16, name="hidden", bufs=2, align_bytes=64)
            for u, (active, bank) in enumerate(pairs):
                nc.vector.tensor_tensor(
                    hidden[:, u * HALF * PACK : (u + 1) * HALF * PACK].rearrange("p (c t) -> p c t", t=PACK),
                    bank[:].rearrange("p t c -> p c t"),
                    active,
                    MULT,
                )
            return quantise(hidden[:], C, "h", 3)

        def second_layer(e, bank):
            acc = bank[:].rearrange("p (nb a) c -> p nb (a c)", nb=2)
            for nb in range(2):
                matmul(acc[:, nb, :], quant["w2", e], slice(nb * P, (nb + 1) * P), quant["h", e], slice(0, C))
            nc.scalar.copy(y_slots[:, :, e * C : (e + 1) * C], acc)

        def scatter(nb, lo, hi):
            nc.vector.tensor_tensor(
                windows[nb][:].indirect(list_cols(lo, hi)), y_slots[:, nb, lo:hi], gates[:, lo:hi], MULT
            )

        nc.sync.dma_start(offsets[:], offs)
        load("w1", 0)
        for r in range(4):
            nc.sync.dma_start(tok_scales[r:P:32, :].bitcast(I32), x_scales[0, r:16:4, :].bitcast(I32))
        nc.sync.dma_start(tok_words[:], x_words[0].rearrange("p t r -> p (t r)").bitcast(I32))
        load("w3", 0)
        for e in range(1, E):
            load("w1", e)
            load("w3", e)
            load_second(e - 1)
        load_second(E - 1)
        residual = {}
        for nb in (1, 0):
            for half in range(2):
                residual[nb, half] = raw_tile("raw_xr")
                cols = slice(half * T // 2, (half + 1) * T // 2)
                nc.sync.dma_start(residual[nb, half][:, 0 : T // 2], xr[nb * P : (nb + 1) * P, cols])

        gather_all()
        prepare("w1", 0)
        prepare("w3", 0)
        done = [0, 0]

        def scatter_ready(e):
            for nb in range(2):
                for hi in SCATTER_ENDS[nb][:-1]:
                    if done[nb] < hi <= (e + 1) * C:
                        scatter(nb, done[nb], hi)
                        done[nb] = hi

        for e in range(E):
            banks = first_layer(e)
            if e + 1 < E:
                prepare("w1", e + 1)
            pairs = activate(e, banks)
            if e + 1 < E:
                prepare("w3", e + 1)
            if e > 0:
                second_layer(e - 1, banks["w1", 0])
            prepare_second(e)
            quant["h", e] = hidden_codes(pairs)
            if e > 0:
                scatter_ready(e - 1)
        second_layer(E - 1, psum.tile([P, PACK, HALF], F32, name="acc_w1", bufs=BANKS["w1"]))
        for nb in (1, 0):
            scatter(nb, done[nb], SLOTS)
            for lo in range(0, T, ADD_COLS):
                half, at = divmod(lo, T // 2)
                res = residual[nb, half][:, at : at + ADD_COLS]
                nc.vector.tensor_tensor(res, res, windows[nb][:, lo : lo + ADD_COLS], ADD)
                nc.sync.dma_start(out[nb * P : (nb + 1) * P, lo : lo + ADD_COLS], res)
